import numpy as np, ml_dtypes
CORES = [8,136,40,168]
N = 4
import mx_ref
NC, NZ = 128, 512
BF = ml_dtypes.bfloat16
def setup_inputs(rng):
    def f(*shape):
        return mx_ref.flush((rng.standard_normal(shape, dtype=np.float32) * np.exp2(rng.integers(-2, 3, shape[:-1] + (1,)))).astype(BF))
    return {"w": f(N, 128, 512), "x": f(N, 128, 4 * NC), "d": f(N, 128, N * 512), "z": f(N, 128, 4 * NZ)}
def setup_inputs_blocks(rng):
    d = setup_inputs(rng)
    for k in ("w", "x", "d", "z"): d[k] = mx_ref.spread(d[k], rng, 1)
    return d
def setup_inputs_wide(rng):
    d = setup_inputs(rng)
    for k in ("w", "x", "d", "z"): d[k] = mx_ref.flush((d[k].astype(np.float32) * np.exp2(rng.integers(-8, 9, (N, 1, 1))).astype(np.float32)).astype(BF))
    return d
def setup_inputs_zeros(rng):
    d = setup_inputs(rng); v = d["x"].reshape(N, 128, -1, 4).copy()
    v[np.broadcast_to((rng.random((N, 1, v.shape[2], 1)) < 0.33), v.shape)] = 0
    d["x"] = v.reshape(d["x"].shape)
    return d
def reference(w, x, d, z):
    QX = [mx_ref.quantize(x[j]) for j in range(N)]; QZ = [mx_ref.quantize(z[j]) for j in range(N)]
    y = np.zeros((N, 128, N * NC), np.float32); h = np.zeros((N, 128, NZ), np.float32)
    for r in range(N):
        qw = mx_ref.quantize(w[r])
        for j in range(N):
            y[r][:, NC * j:NC * j + NC] = mx_ref.matmul(qw, QX[j])
            p = mx_ref.matmul(mx_ref.quantize(d[r][:, 512 * j:512 * j + 512]), QZ[j])
            h[r] = p if j == 0 else h[r] + p
    return {"y": y, "h": h}

@@ -1,0 +1,175 @@
+from concourse.mybir import dt, ActivationFunctionType
+
+N = 4
+ZW, XW = 512, 128
+SLOT = ZW + XW
+HALF = ZW // 2
+
+SCRATCH = {
+    "xt": ("sbuf", [128, 4 * XW], "bfloat16"),
+    "zt": ("sbuf", [128, 4 * ZW], "bfloat16"),
+    "wt": ("sbuf", [128, 512], "bfloat16"),
+    "dtile": ("sbuf", [128, N * 512], "bfloat16"),
+    "codes": ("sbuf", [128, N * SLOT], "float8_e4m3fn_x4"),
+    "planes": ("sbuf", [128, N * SLOT], "uint8"),
+    "wc": ("sbuf", [128, 128], "float8_e4m3fn_x4"),
+    "ws": ("sbuf", [128, 128], "uint8"),
+    "dc": ("sbuf", [128, N * 128], "float8_e4m3fn_x4"),
+    "ds": ("sbuf", [128, N * 128], "uint8"),
+    "ysb": ("sbuf", [128, N * 128], "float32"),
+    "hsb": ("sbuf", [128, ZW], "float32"),
+    "py": ("psum", [128, N * 512], "float32"),
+    "ph": ("psum", [128, 2 * 512], "float32"),
+}
+
+PIECES = {
+    "cx": ("c", ZW, SLOT, ("qx",)),
+    "s": ("s", 0, SLOT, ("qx", "qz")),
+    "cz": ("c", 0, ZW, ("qz",)),
+}
+PLAN = [
+    ("cx", 0, "all"),
+    ("s", 1, "chip_only"),
+    ("cz", None, None),
+]
+NEED_H = ("s", "cz")
+NEED_Y = ("s", "cx")
+
+SEMAPHORES = (["lx", "lz", "lw", "ld", "qx", "qz", "qw", "qd", "hin", "sent", "hm0", "hm1", "yc", "hc", "st"]
+              + ["ym%d" % k for k in range(N)]
+              + ["a_%s%d" % (p, j) for p in PIECES for j in range(N)])
+
+
+def _count(mask):
+    return bin(mask).count("1")
+
+
+def _helpers(R, T, topo):
+    world = range((max(topo.host(c) for c in T.cores) + 1) * topo.CORES_PER_HOST)
+    here = [c for c in world if c != R and topo.host(c) == topo.host(R) and topo.chip(c) == topo.chip(R)
+            and T.rank_of(c) is None and all(topo.may_write(c, p) for p in T.cores if p != R)]
+    return [c for c in here if topo.die(c) != topo.die(R)] + [c for c in here if topo.die(c) == topo.die(R)]
+
+
+def _view(T, piece, r):
+    kind, lo, hi, _ = PIECES[piece]
+    if kind == "c":
+        return T.codes[:, r * SLOT + lo:r * SLOT + hi].bitcast(dt.uint8)
+    return T.planes[:, r * SLOT + lo:r * SLOT + hi]
+
+
+def _to_peers(g, T, topo, me, r, piece):
+    n = 0
+    for k in range(1, N):
+        dst = T.cores[(r + k) % N]
+        rid, pid = topo.addr(dst, me)
+        m = topo.mask(me, dst)
+        g.remote_dma(out_ap=_view(T, piece, r), in_ap=_view(T, piece, r), remote_sem=T.sem["a_%s%d" % (piece, r)],
+                     local_sem=T.sem.sent, pid=pid, routing_id=rid, dma_engine_mask=m)
+        n += _count(m)
+    return n
+
+
+def _handover_mask(topo, R, H, peer, how):
+    m = topo.mask(R, H)
+    if how == "chip_only":
+        m &= ~topo.mask(R, peer)
+    return m
+
+
+def rank_program(g, core, T, topo):
+    S = T.sem
+    rank = T.rank_of(core)
+    if rank is None:
+        for r, R in enumerate(T.cores):
+            hs = _helpers(R, T, topo)
+            for piece, via, how in PLAN:
+                if via is not None and hs[via] == core:
+                    g.wait_ge(S.hin, _count(_handover_mask(topo, R, core, T.cores[(r + 1) % N], how)))
+                    g.wait_ge(S.sent, _to_peers(g, T, topo, core, r, piece))
+        return
+
+    v, te, sc, sy = g.vector, g.tensor, g.scalar, g.sync
+    own = rank * SLOT
+    hs = _helpers(core, T, topo)
+
+    sy.dma_start(T.xt[:], T.x[:]).then_inc(S.lx, 16)
+    sy.dma_start(T.zt[:], T.z[:]).then_inc(S.lz, 16)
+    sy.dma_start(T.wt[:], T.w[:]).then_inc(S.lw, 16)
+    sy.dma_start(T.dtile[:], T.d[:]).then_inc(S.ld, 16)
+
+    v.wait_ge(S.lx, 16)
+    v.quantize_mx(T.codes[:, own + ZW:own + SLOT], T.planes[:, own + ZW:own + SLOT], T.xt[:]).then_inc(S.qx, 1)
+    v.wait_ge(S.lz, 16)
+    v.quantize_mx(T.codes[:, own:own + ZW], T.planes[:, own:own + ZW], T.zt[:]).then_inc(S.qz, 1)
+    v.wait_ge(S.lw, 16)
+    v.quantize_mx(T.wc[:], T.ws[:], T.wt[:]).then_inc(S.qw, 1)
+    v.wait_ge(S.ld, 16)
+    v.quantize_mx(T.dc[:], T.ds[:], T.dtile[:]).then_inc(S.qd, 1)
+
+    sent = 0
+    for piece, via, how in PLAN:
+        for q in PIECES[piece][3]:
+            g.wait_ge(S[q], 1)
+        if via is None:
+            sent += _to_peers(g, T, topo, core, rank, piece)
+        else:
+            H = hs[via]
+            rid, pid = topo.addr(H, core)
+            m = _handover_mask(topo, core, H, T.cores[(rank + 1) % N], how)
+            g.remote_dma(out_ap=_view(T, piece, rank), in_ap=_view(T, piece, rank), remote_sem=S.hin,
+                         local_sem=S.sent, pid=pid, routing_id=rid, dma_engine_mask=m)
+            sent += _count(m)
+    g.wait_ge(S.sent, sent)
+
+    def arrived(j, pieces):
+        for piece, via, how in PLAN:
+            if piece in pieces:
+                src = T.cores[j] if via is None else _helpers(T.cores[j], T, topo)[via]
+                te.wait_ge(S["a_%s%d" % (piece, j)], _count(topo.mask(src, core)))
+
+    def h_slice(j, first, last):
+        for b in range(2):
+            c0 = j * SLOT + b * HALF
+            i = te.matmul_mx(T.ph[:, 512 * b:512 * b + HALF], T.dc[:, 128 * j:128 * j + 128], T.ds[:, 128 * j:128 * j + 128],
+                             T.codes[:, c0:c0 + HALF], T.planes[:, c0:c0 + HALF], first, last)
+            if last:
+                i.then_inc(S["hm%d" % b], 1)
+
+    def y_block(j, k):
+        c0 = j * SLOT + ZW
+        te.matmul_mx(T.py[:, 512 * k:512 * k + XW], T.wc[:], T.ws[:], T.codes[:, c0:c0 + XW], T.planes[:, c0:c0 + XW],
+                     True, True).then_inc(S["ym%d" % k], 1)
+
+    te.wait_ge(S.qx, 1)
+    te.wait_ge(S.qw, 1)
+    y_block(rank, 0)
+    te.wait_ge(S.qz, 1)
+    te.wait_ge(S.qd, 1)
+    h_slice(rank, True, False)
+    for k in range(1, N):
+        j = (rank - k) % N
+        arrived(j, NEED_H)
+        h_slice(j, False, k == N - 1)
+        arrived(j, NEED_Y)
+        y_block(j, k)
+
+    def ycols(k):
+        j = (rank - k) % N
+        return T.ysb[:, XW * j:XW * j + XW]
+
+    for k in range(N - 1):
+        sc.wait_ge(S["ym%d" % k], 1)
+        sc.activation(ycols(k), T.py[:, 512 * k:512 * k + XW], ActivationFunctionType.Copy).then_inc(S.yc, 1)
+    sc.wait_ge(S.hm1, 1)
+    sc.activation(T.hsb[:, HALF:ZW], T.ph[:, 512:512 + HALF], ActivationFunctionType.Copy).then_inc(S.hc, 1)
+    v.wait_ge(S.hm0, 1)
+    v.tensor_copy(T.hsb[:, 0:HALF], T.ph[:, 0:HALF]).then_inc(S.hc, 1)
+    v.wait_ge(S["ym%d" % (N - 1)], 1)
+    v.tensor_copy(ycols(N - 1), T.py[:, 512 * (N - 1):512 * (N - 1) + XW]).then_inc(S.yc, 1)
+
+    sc.wait_ge(S.hc, 2)
+    sc.dma_start(T.h[:], T.hsb[:]).then_inc(S.st, 16)
+    sy.wait_ge(S.yc, N)
+    sy.dma_start(T.y[:], T.ysb[:]).then_inc(S.st, 16)
+    sy.wait_ge(S.st, 32)

@@ -1,9 +1,10 @@
+from concourse.bass import DstId, RemoteDMATransfer
 from concourse.mybir import dt, ActivationFunctionType
 
 N = 4
 ZW, XW = 512, 128
 SLOT = ZW + XW
-HALF = ZW // 2
+BANKS = ((0, 192), (192, 192), (384, 128))
 
 SCRATCH = {
     "xt": ("sbuf", [128, 4 * XW], "bfloat16"),
@@ -19,24 +20,28 @@ SCRATCH = {
     "ysb": ("sbuf", [128, N * 128], "float32"),
     "hsb": ("sbuf", [128, ZW], "float32"),
     "py": ("psum", [128, N * 512], "float32"),
-    "ph": ("psum", [128, 2 * 512], "float32"),
+    "ph": ("psum", [128, len(BANKS) * 512], "float32"),
 }
 
 PIECES = {
-    "cx": ("c", ZW, SLOT, ("qx",)),
-    "s": ("s", 0, SLOT, ("qx", "qz")),
-    "cz": ("c", 0, ZW, ("qz",)),
+    "cx": ("c", ZW, SLOT, "qx"),
+    "sx": ("s", ZW, SLOT, "qx"),
+    "sz": ("s", 0, ZW, "qz"),
+    "cz": ("c", 0, ZW, "qz"),
 }
+EACH = ((1, (1,)), (2, (2,)), (3, (3,)))
 PLAN = [
-    ("cx", 0, "all"),
-    ("s", 1, "chip_only"),
-    ("cz", None, None),
+    ("cx", ((0, (1, 2, 3)),), "all"),
+    ("sx", EACH, "chip_only"),
+    ("cz", ((None, (1,)),), None),
+    ("sz", EACH, "chip_only"),
+    ("cz", ((None, (2, 3)),), None),
 ]
-NEED_H = ("s", "cz")
-NEED_Y = ("s", "cx")
+NEED_H = ("sz", "cz")
+NEED_Y = ("sx", "cx")
 
-SEMAPHORES = (["lx", "lz", "lw", "ld", "qx", "qz", "qw", "qd", "hin", "sent", "hm0", "hm1", "yc", "hc", "st"]
-              + ["ym%d" % k for k in range(N)]
+SEMAPHORES = (["lx", "lz", "lw", "ld", "qx", "qz", "qw", "qd", "sent", "yc", "hc", "st"]
+              + ["ym%d" % k for k in range(N)] + ["hm%d" % b for b in range(len(BANKS))] + ["h_%s" % p for p in PIECES]
               + ["a_%s%d" % (p, j) for p in PIECES for j in range(N)])
 
 
@@ -58,9 +63,9 @@ def _view(T, piece, r):
     return T.planes[:, r * SLOT + lo:r * SLOT + hi]
 
 
-def _to_peers(g, T, topo, me, r, piece):
+def _to_peers(g, T, topo, me, r, piece, steps):
     n = 0
-    for k in range(1, N):
+    for k in steps:
         dst = T.cores[(r + k) % N]
         rid, pid = topo.addr(dst, me)
         m = topo.mask(me, dst)
@@ -81,12 +86,16 @@ def rank_program(g, core, T, topo):
     S = T.sem
     rank = T.rank_of(core)
     if rank is None:
+        sent = 0
         for r, R in enumerate(T.cores):
             hs = _helpers(R, T, topo)
-            for piece, via, how in PLAN:
-                if via is not None and hs[via] == core:
-                    g.wait_ge(S.hin, _count(_handover_mask(topo, R, core, T.cores[(r + 1) % N], how)))
-                    g.wait_ge(S.sent, _to_peers(g, T, topo, core, r, piece))
+            for piece, carriers, how in PLAN:
+                for via, steps in carriers:
+                    if via is not None and hs[via] == core:
+                        g.wait_ge(S["h_" + piece], _count(_handover_mask(topo, R, core, T.cores[(r + 1) % N], how)))
+                        sent += _to_peers(g, T, topo, core, r, piece, steps)
+        if sent:
+            g.wait_ge(S.sent, sent)
         return
 
     v, te, sc, sy = g.vector, g.tensor, g.scalar, g.sync
@@ -94,7 +103,7 @@ def rank_program(g, core, T, topo):
     hs = _helpers(core, T, topo)
 
     sy.dma_start(T.xt[:], T.x[:]).then_inc(S.lx, 16)
-    sy.dma_start(T.zt[:], T.z[:]).then_inc(S.lz, 16)
+    sc.dma_start(T.zt[:], T.z[:]).then_inc(S.lz, 16)
     sy.dma_start(T.wt[:], T.w[:]).then_inc(S.lw, 16)
     sy.dma_start(T.dtile[:], T.d[:]).then_inc(S.ld, 16)
 
@@ -108,31 +117,32 @@ def rank_program(g, core, T, topo):
     v.quantize_mx(T.dc[:], T.ds[:], T.dtile[:]).then_inc(S.qd, 1)
 
     sent = 0
-    for piece, via, how in PLAN:
-        for q in PIECES[piece][3]:
-            g.wait_ge(S[q], 1)
-        if via is None:
-            sent += _to_peers(g, T, topo, core, rank, piece)
+    for piece, carriers, how in PLAN:
+        g.wait_ge(S[PIECES[piece][3]], 1)
+        if carriers[0][0] is None:
+            sent += _to_peers(g, T, topo, core, rank, piece, carriers[0][1])
         else:
-            H = hs[via]
-            rid, pid = topo.addr(H, core)
-            m = _handover_mask(topo, core, H, T.cores[(rank + 1) % N], how)
-            g.remote_dma(out_ap=_view(T, piece, rank), in_ap=_view(T, piece, rank), remote_sem=S.hin,
-                         local_sem=S.sent, pid=pid, routing_id=rid, dma_engine_mask=m)
+            H = [hs[via] for via, steps in carriers]
+            m = _handover_mask(topo, core, H[0], T.cores[(rank + 1) % N], how)
+            ids = [topo.addr(h, core) for h in H]
+            g.remote_dma_fused([RemoteDMATransfer(dst_ids=[DstId(rid=rid, pnc=pid) for rid, pid in ids], dma_engine_mask=m,
+                                                  remote_sem=S["h_" + piece], srcs=[_view(T, piece, rank)],
+                                                  dsts=[_view(T, piece, rank) for h in H])], local_sem=S.sent)
             sent += _count(m)
     g.wait_ge(S.sent, sent)
 
     def arrived(j, pieces):
-        for piece, via, how in PLAN:
-            if piece in pieces:
-                src = T.cores[j] if via is None else _helpers(T.cores[j], T, topo)[via]
-                te.wait_ge(S["a_%s%d" % (piece, j)], _count(topo.mask(src, core)))
+        for piece, carriers, how in PLAN:
+            for via, steps in carriers:
+                if piece in pieces and (rank - j) % N in steps:
+                    src = T.cores[j] if via is None else _helpers(T.cores[j], T, topo)[via]
+                    te.wait_ge(S["a_%s%d" % (piece, j)], _count(topo.mask(src, core)))
 
     def h_slice(j, first, last):
-        for b in range(2):
-            c0 = j * SLOT + b * HALF
-            i = te.matmul_mx(T.ph[:, 512 * b:512 * b + HALF], T.dc[:, 128 * j:128 * j + 128], T.ds[:, 128 * j:128 * j + 128],
-                             T.codes[:, c0:c0 + HALF], T.planes[:, c0:c0 + HALF], first, last)
+        for b, (lo, n) in enumerate(BANKS):
+            c0 = j * SLOT + lo
+            i = te.matmul_mx(T.ph[:, 512 * b:512 * b + n], T.dc[:, 128 * j:128 * j + 128], T.ds[:, 128 * j:128 * j + 128],
+                             T.codes[:, c0:c0 + n], T.planes[:, c0:c0 + n], first, last)
             if last:
                 i.then_inc(S["hm%d" % b], 1)
 
@@ -149,27 +159,26 @@ def rank_program(g, core, T, topo):
     h_slice(rank, True, False)
     for k in range(1, N):
         j = (rank - k) % N
-        arrived(j, NEED_H)
-        h_slice(j, False, k == N - 1)
         arrived(j, NEED_Y)
         y_block(j, k)
+        arrived(j, NEED_H)
+        h_slice(j, False, k == N - 1)
 
-    def ycols(k):
+    for k in range(N):
         j = (rank - k) % N
-        return T.ysb[:, XW * j:XW * j + XW]
-
-    for k in range(N - 1):
         sc.wait_ge(S["ym%d" % k], 1)
-        sc.activation(ycols(k), T.py[:, 512 * k:512 * k + XW], ActivationFunctionType.Copy).then_inc(S.yc, 1)
-    sc.wait_ge(S.hm1, 1)
-    sc.activation(T.hsb[:, HALF:ZW], T.ph[:, 512:512 + HALF], ActivationFunctionType.Copy).then_inc(S.hc, 1)
-    v.wait_ge(S.hm0, 1)
-    v.tensor_copy(T.hsb[:, 0:HALF], T.ph[:, 0:HALF]).then_inc(S.hc, 1)
-    v.wait_ge(S["ym%d" % (N - 1)], 1)
-    v.tensor_copy(ycols(N - 1), T.py[:, 512 * (N - 1):512 * (N - 1) + XW]).then_inc(S.yc, 1)
+        sc.activation(T.ysb[:, XW * j:XW * j + XW], T.py[:, 512 * k:512 * k + XW],
+                      ActivationFunctionType.Copy).then_inc(S.yc, 1)
+    for b, (lo, n) in enumerate(BANKS):
+        if b == 1:
+            sc.wait_ge(S["hm%d" % b], 1)
+            sc.activation(T.hsb[:, lo:lo + n], T.ph[:, 512 * b:512 * b + n], ActivationFunctionType.Copy).then_inc(S.hc, 1)
+        else:
+            v.wait_ge(S["hm%d" % b], 1)
+            v.tensor_copy(T.hsb[:, lo:lo + n], T.ph[:, 512 * b:512 * b + n]).then_inc(S.hc, 1)
 
-    sc.wait_ge(S.hc, 2)
-    sc.dma_start(T.h[:], T.hsb[:]).then_inc(S.st, 16)
     sy.wait_ge(S.yc, N)
     sy.dma_start(T.y[:], T.ysb[:]).then_inc(S.st, 16)
+    sc.wait_ge(S.hc, len(BANKS))
+    sc.dma_start(T.h[:], T.hsb[:]).then_inc(S.st, 16)
     sy.wait_ge(S.st, 32)

from concourse.bass import DstId, RemoteDMATransfer
from concourse.mybir import dt, ActivationFunctionType

N = 4
ZW, XW = 512, 128
SLOT = ZW + XW
BANKS = ((0, 192), (192, 192), (384, 128))

SCRATCH = {
    "xt": ("sbuf", [128, 4 * XW], "bfloat16"),
    "zt": ("sbuf", [128, 4 * ZW], "bfloat16"),
    "wt": ("sbuf", [128, 512], "bfloat16"),
    "dtile": ("sbuf", [128, N * 512], "bfloat16"),
    "codes": ("sbuf", [128, N * SLOT], "float8_e4m3fn_x4"),
    "planes": ("sbuf", [128, N * SLOT], "uint8"),
    "wc": ("sbuf", [128, 128], "float8_e4m3fn_x4"),
    "ws": ("sbuf", [128, 128], "uint8"),
    "dc": ("sbuf", [128, N * 128], "float8_e4m3fn_x4"),
    "ds": ("sbuf", [128, N * 128], "uint8"),
    "ysb": ("sbuf", [128, N * 128], "float32"),
    "hsb": ("sbuf", [128, ZW], "float32"),
    "py": ("psum", [128, N * 512], "float32"),
    "ph": ("psum", [128, len(BANKS) * 512], "float32"),
}

PIECES = {
    "cx": ("c", ZW, SLOT, "qx"),
    "sx": ("s", ZW, SLOT, "qx"),
    "sz": ("s", 0, ZW, "qz"),
    "cz": ("c", 0, ZW, "qz"),
}
EACH = ((1, (1,)), (2, (2,)), (3, (3,)))
PLAN = [
    ("cx", ((0, (1, 2, 3)),), "all"),
    ("sx", EACH, "chip_only"),
    ("cz", ((None, (1,)),), None),
    ("sz", EACH, "chip_only"),
    ("cz", ((None, (2, 3)),), None),
]
NEED_H = ("sz", "cz")
NEED_Y = ("sx", "cx")

SEMAPHORES = (["lx", "lz", "lw", "ld", "qx", "qz", "qw", "qd", "sent", "yc", "hc", "st"]
              + ["ym%d" % k for k in range(N)] + ["hm%d" % b for b in range(len(BANKS))] + ["h_%s" % p for p in PIECES]
              + ["a_%s%d" % (p, j) for p in PIECES for j in range(N)])


def _count(mask):
    return bin(mask).count("1")


def _helpers(R, T, topo):
    world = range((max(topo.host(c) for c in T.cores) + 1) * topo.CORES_PER_HOST)
    here = [c for c in world if c != R and topo.host(c) == topo.host(R) and topo.chip(c) == topo.chip(R)
            and T.rank_of(c) is None and all(topo.may_write(c, p) for p in T.cores if p != R)]
    return [c for c in here if topo.die(c) != topo.die(R)] + [c for c in here if topo.die(c) == topo.die(R)]


def _view(T, piece, r):
    kind, lo, hi, _ = PIECES[piece]
    if kind == "c":
        return T.codes[:, r * SLOT + lo:r * SLOT + hi].bitcast(dt.uint8)
    return T.planes[:, r * SLOT + lo:r * SLOT + hi]


def _to_peers(g, T, topo, me, r, piece, steps):
    n = 0
    for k in steps:
        dst = T.cores[(r + k) % N]
        rid, pid = topo.addr(dst, me)
        m = topo.mask(me, dst)
        g.remote_dma(out_ap=_view(T, piece, r), in_ap=_view(T, piece, r), remote_sem=T.sem["a_%s%d" % (piece, r)],
                     local_sem=T.sem.sent, pid=pid, routing_id=rid, dma_engine_mask=m)
        n += _count(m)
    return n


def _handover_mask(topo, R, H, peer, how):
    m = topo.mask(R, H)
    if how == "chip_only":
        m &= ~topo.mask(R, peer)
    return m


def rank_program(g, core, T, topo):
    S = T.sem
    rank = T.rank_of(core)
    if rank is None:
        sent = 0
        for r, R in enumerate(T.cores):
            hs = _helpers(R, T, topo)
            for piece, carriers, how in PLAN:
                for via, steps in carriers:
                    if via is not None and hs[via] == core:
                        g.wait_ge(S["h_" + piece], _count(_handover_mask(topo, R, core, T.cores[(r + 1) % N], how)))
                        sent += _to_peers(g, T, topo, core, r, piece, steps)
        if sent:
            g.wait_ge(S.sent, sent)
        return

    v, te, sc, sy = g.vector, g.tensor, g.scalar, g.sync
    own = rank * SLOT
    hs = _helpers(core, T, topo)

    sy.dma_start(T.xt[:], T.x[:]).then_inc(S.lx, 16)
    sc.dma_start(T.zt[:], T.z[:]).then_inc(S.lz, 16)
    sy.dma_start(T.wt[:], T.w[:]).then_inc(S.lw, 16)
    sy.dma_start(T.dtile[:], T.d[:]).then_inc(S.ld, 16)

    v.wait_ge(S.lx, 16)
    v.quantize_mx(T.codes[:, own + ZW:own + SLOT], T.planes[:, own + ZW:own + SLOT], T.xt[:]).then_inc(S.qx, 1)
    v.wait_ge(S.lz, 16)
    v.quantize_mx(T.codes[:, own:own + ZW], T.planes[:, own:own + ZW], T.zt[:]).then_inc(S.qz, 1)
    v.wait_ge(S.lw, 16)
    v.quantize_mx(T.wc[:], T.ws[:], T.wt[:]).then_inc(S.qw, 1)
    v.wait_ge(S.ld, 16)
    v.quantize_mx(T.dc[:], T.ds[:], T.dtile[:]).then_inc(S.qd, 1)

    sent = 0
    for piece, carriers, how in PLAN:
        g.wait_ge(S[PIECES[piece][3]], 1)
        if carriers[0][0] is None:
            sent += _to_peers(g, T, topo, core, rank, piece, carriers[0][1])
        else:
            H = [hs[via] for via, steps in carriers]
            m = _handover_mask(topo, core, H[0], T.cores[(rank + 1) % N], how)
            ids = [topo.addr(h, core) for h in H]
            g.remote_dma_fused([RemoteDMATransfer(dst_ids=[DstId(rid=rid, pnc=pid) for rid, pid in ids], dma_engine_mask=m,
                                                  remote_sem=S["h_" + piece], srcs=[_view(T, piece, rank)],
                                                  dsts=[_view(T, piece, rank) for h in H])], local_sem=S.sent)
            sent += _count(m)
    g.wait_ge(S.sent, sent)

    def arrived(j, pieces):
        for piece, carriers, how in PLAN:
            for via, steps in carriers:
                if piece in pieces and (rank - j) % N in steps:
                    src = T.cores[j] if via is None else _helpers(T.cores[j], T, topo)[via]
                    te.wait_ge(S["a_%s%d" % (piece, j)], _count(topo.mask(src, core)))

    def h_slice(j, first, last):
        for b, (lo, n) in enumerate(BANKS):
            c0 = j * SLOT + lo
            i = te.matmul_mx(T.ph[:, 512 * b:512 * b + n], T.dc[:, 128 * j:128 * j + 128], T.ds[:, 128 * j:128 * j + 128],
                             T.codes[:, c0:c0 + n], T.planes[:, c0:c0 + n], first, last)
            if last:
                i.then_inc(S["hm%d" % b], 1)

    def y_block(j, k):
        c0 = j * SLOT + ZW
        te.matmul_mx(T.py[:, 512 * k:512 * k + XW], T.wc[:], T.ws[:], T.codes[:, c0:c0 + XW], T.planes[:, c0:c0 + XW],
                     True, True).then_inc(S["ym%d" % k], 1)

    te.wait_ge(S.qx, 1)
    te.wait_ge(S.qw, 1)
    y_block(rank, 0)
    te.wait_ge(S.qz, 1)
    te.wait_ge(S.qd, 1)
    h_slice(rank, True, False)
    for k in range(1, N):
        j = (rank - k) % N
        arrived(j, NEED_Y)
        y_block(j, k)
        arrived(j, NEED_H)
        h_slice(j, False, k == N - 1)

    for k in range(N):
        j = (rank - k) % N
        sc.wait_ge(S["ym%d" % k], 1)
        sc.activation(T.ysb[:, XW * j:XW * j + XW], T.py[:, 512 * k:512 * k + XW],
                      ActivationFunctionType.Copy).then_inc(S.yc, 1)
    for b, (lo, n) in enumerate(BANKS):
        if b == 1:
            sc.wait_ge(S["hm%d" % b], 1)
            sc.activation(T.hsb[:, lo:lo + n], T.ph[:, 512 * b:512 * b + n], ActivationFunctionType.Copy).then_inc(S.hc, 1)
        else:
            v.wait_ge(S["hm%d" % b], 1)
            v.tensor_copy(T.hsb[:, lo:lo + n], T.ph[:, 512 * b:512 * b + n]).then_inc(S.hc, 1)

    sy.wait_ge(S.yc, N)
    sy.dma_start(T.y[:], T.ysb[:]).then_inc(S.st, 16)
    sc.wait_ge(S.hc, len(BANKS))
    sc.dma_start(T.h[:], T.hsb[:]).then_inc(S.st, 16)
    sy.wait_ge(S.st, 32)
